import numpy as np
import ml_dtypes


def mxq(x, axis, fmt="e4m3"):
    dtype, down = {"e4m3": (ml_dtypes.float8_e4m3fn, 7), "e5m2": (ml_dtypes.float8_e5m2, 14)}[fmt]
    v = np.moveaxis(np.asarray(x, np.float32).astype(ml_dtypes.bfloat16).astype(np.float64), axis, -1)
    blocks = v.reshape(v.shape[:-1] + (-1, 32))
    amax = np.abs(blocks).max(-1, keepdims=True)
    byte = np.maximum(np.where(amax > 0, np.frexp(amax)[1] - 1 + 127, 0) - down, 1)
    scale = np.exp2(byte - 127.0)
    codes = (blocks / scale).astype(np.float32).astype(dtype).astype(np.float64)
    return np.moveaxis((codes * scale).reshape(v.shape), -1, axis)


WIDE = False


def mx_kscale(k):
    if not WIDE:
        return np.ones(k)
    levels = np.array([10, -10, 5, -5, 0])
    if k % 512:
        return np.exp2(np.random.permutation(np.resize(levels, k // 32))).repeat(32)
    a = np.empty((k // 512, 16))
    for p in range(k // 512):
        a[p, :8] = np.random.permutation(np.resize(levels, 8))
        for g in range(8):
            far = levels[np.abs(levels - a[p, g]) >= 10]
            a[p, g + 8] = far[np.random.randint(len(far))]
    return np.exp2(a.ravel()).repeat(32)


def f64(x):
    return np.asarray(x).astype(np.float64)


def striped(idx):
    return np.tile(idx.reshape(-1, 16).T, (8, 1)).astype(np.uint16)


def unstriped(offs):
    return offs[:16].T.reshape(-1).astype(np.int64)


def pack_weight(w):
    k, n = w.shape
    w = f64(np.asarray(w, np.float32).astype(ml_dtypes.bfloat16)).reshape(k // 32, 32, n)
    amax = np.abs(w).max(1)
    byte = np.clip(np.where(amax > 0, np.frexp(amax)[1] - 1 + 127 - 7, 1), 1, 254)
    scaled = (w * np.exp2(127.0 - byte)[:, None, :]).reshape(k, n).astype(np.float32)
    words = np.ascontiguousarray(scaled.reshape(k // 512, 128, 4, n).transpose(0, 1, 3, 2)).astype(ml_dtypes.float8_e4m3fn).view(np.uint8)
    return words, np.ascontiguousarray(byte.astype(np.uint8).reshape(k // 512, 16, n))


def unpack_weight(words, scales):
    g, p, n, _ = words.shape
    vals = np.ascontiguousarray(words).view(ml_dtypes.float8_e4m3fn).astype(np.float64) * np.repeat(np.exp2(scales.astype(np.float64) - 127.0), 8, axis=1)[..., None]
    return vals.transpose(0, 1, 3, 2).reshape(g * 512, n)


def planes(y):
    n, m = y.shape
    v = y.astype(np.float32).astype(ml_dtypes.bfloat16).astype(np.float64).reshape(n // 32, 32, m)
    top = np.abs(v).max(1)
    byte = np.clip(np.where(top > 0, np.frexp(top)[1] - 1 + 127 - 7, 1), 1, 254)
    codes = (v * np.exp2(127.0 - byte)[:, None, :]).reshape(n, m).astype(np.float32).astype(ml_dtypes.float8_e4m3fn).view(np.uint8)
    words = codes.reshape(n // 512, 128, 4, m).transpose(0, 1, 3, 2)
    return np.ascontiguousarray(words), np.ascontiguousarray(byte.astype(np.uint8).reshape(n // 512, 16, m))


K, T, S, H, N = 512, 1024, 512, 512, 512


def setup_inputs():
    n = np.random.standard_normal
    s = mx_kscale(K)[:, None]
    u = mx_kscale(H)
    packed_xT = pack_weight(n((K, T)) * s)
    return {
        "x_words": packed_xT[0],
        "x_scales": packed_xT[1],
        "w1": (n((K, N)) / np.sqrt(K) / s).astype(np.float32),
        "dual": (n((H, S))).astype(np.float32),
        "low": (-np.random.uniform(0.2, 1.0, (H, S))).astype(np.float32),
        "high": (np.random.uniform(0.2, 1.0, (H, S))).astype(np.float32),
        "rho": (np.random.uniform(0.5, 1.5, (H, 1)) * u[:, None]).astype(np.float32),
        "w2": (n((H, N)) / np.sqrt(H) / u[:, None]).astype(np.float32),
        "lin": (n((N, S))).astype(np.float32),
        "offs": striped(np.random.permutation(T)[:S]),
    }


def reference(x_words, x_scales, w1, dual, low, high, rho, w2, lin, offs):
    xq = unpack_weight(x_words, x_scales)[:, unstriped(offs)]
    y = mxq(f64(w1), 0, "e4m3").T @ xq
    t0 = y + 0.5 * f64(dual)
    clip = np.minimum(np.maximum(t0, f64(low)), f64(high))
    dn = 2.0 * (t0 - clip)
    rr = f64(rho) * (2.0 * clip - dn)
    out_0 = (mxq(f64(w2), 0, "e4m3").T @ mxq(rr, 0, "e4m3")) + f64(lin)
    return (out_0,) + planes(out_0)

@@ -1,0 +1,163 @@
+from contextlib import ExitStack
+
+import concourse.mybir as mybir
+
+K, T, S, H, N = 512, 1024, 512, 512, 512
+FLOPS = 2 * K * H * S + 2 * H * N * S
+
+F32 = mybir.dt.float32
+BF16 = mybir.dt.bfloat16
+I32 = mybir.dt.int32
+U32 = mybir.dt.uint32
+U16 = mybir.dt.uint16
+U8 = mybir.dt.uint8
+FP8X4 = mybir.dt.float8_e4m3fn_x4
+ALU = mybir.AluOpType
+COPY = mybir.ActivationFunctionType.Copy
+
+P = 128
+PACK = 4
+QUADS = 4
+HALF = S // 2
+CHUNK = 128
+RUN = 4
+W2_PIECES = 4
+
+
+def tile_picked_yosqp_x_po_kernel(
+    tc, x_words, x_scales, w1, dual, low, high, rho, w2, lin, offs, out_0, out_1, out_2
+):
+    nc = tc.nc
+    with ExitStack() as ctx:
+        held = ctx.enter_context(tc.tile_pool(name="held", bufs=1))
+        psum = ctx.enter_context(tc.psum_pool(name="psum", bufs=1))
+
+        def sbuf(name, shape, dtype):
+            return held.tile(shape, dtype, name=name, align_bytes=64)
+
+        def dealt(matrix):
+            return matrix.rearrange("(p t) c -> p t c", t=PACK)
+
+        def interleave(copy, dst, src):
+            copy(
+                out=dst.rearrange("p (c i t) -> p c t i", i=RUN, t=PACK),
+                in_=src.rearrange("p t (c i) -> p c t i", i=RUN),
+            )
+
+        offsets = held.tile([P, S // 16], U16, name="offsets")
+        table_words = sbuf("table_words", [P, T], U32)
+        table_scales = sbuf("table_scales", [P, T], U8)
+        nc.vector.memset(table_scales[:].bitcast(I32), 0)
+        nc.sync.dma_start(offsets[:], offs)
+        nc.sync.dma_start(table_words[:].bitcast(I32), x_words[0].rearrange("p c t -> p (c t)").bitcast(I32))
+        for q in range(QUADS):
+            nc.sync.dma_start(
+                table_scales[32 * q : 32 * q + 4, :].bitcast(I32), x_scales[0, 4 * q : 4 * q + 4, :].bitcast(I32)
+            )
+        w1_raw = sbuf("w1_raw", [P, PACK, H], F32)
+        nc.sync.dma_start(w1_raw[:], dealt(w1))
+
+        dual_sb, low_sb, high_sb = [], [], []
+        rho_sb = sbuf("rho_sb", [P, PACK], F32)
+        w2_raw = sbuf("w2_raw", [P, PACK, N], F32)
+        for t in range(PACK):
+            for name, matrix, tiles in (("dual", dual, dual_sb), ("low", low, low_sb), ("high", high, high_sb)):
+                tiles.append(sbuf("%s%d" % (name, t), [P, S], F32))
+                nc.sync.dma_start(tiles[t][:], dealt(matrix)[:, t, :])
+            if t == 0:
+                nc.sync.dma_start(rho_sb[:], rho.rearrange("(p t) o -> p (t o)", t=PACK))
+            if t == 1:
+                nc.sync.dma_start(w2_raw[:], dealt(w2))
+        lin_sb = []
+        for h in range(2):
+            lin_sb.append(sbuf("lin%d" % h, [P, PACK, HALF], F32))
+            nc.sync.dma_start(lin_sb[h][:], dealt(lin)[:, :, h * HALF : (h + 1) * HALF])
+
+        x_codes = sbuf("x_codes", [P, S], U32)
+        x_plane = sbuf("x_plane", [P, S], U8)
+        nc.vector.tensor_copy(x_plane[:], table_scales[:].indirect(offsets[:]))
+        nc.vector.tensor_copy(x_codes[:], table_words[:].indirect(offsets[:]))
+
+        w1_first = sbuf("w1_first", [P, P * PACK], BF16)
+        w1_rest = sbuf("w1_rest", [P, PACK - 1, P * PACK], BF16)
+        w1_cols = w1_raw[:].rearrange("p j (m t) -> p m j t", t=PACK)
+        nc.vector.tensor_copy(out=w1_first[:].rearrange("p (m j) -> p m j", j=PACK), in_=w1_cols[:, :, :, 0])
+        nc.scalar.copy(out=w1_rest[:].rearrange("p t (m j) -> p m j t", j=PACK), in_=w1_cols[:, :, :, 1:])
+        w1_codes = [sbuf("w1_codes%d" % t, [P, P], U32) for t in range(PACK)]
+        w1_plane = [sbuf("w1_plane%d" % t, [P, P], U8) for t in range(PACK)]
+
+        rho2 = sbuf("rho2", [P, PACK], F32)
+        rho4 = sbuf("rho4", [P, PACK], F32)
+        nc.scalar.activation(rho2[:], rho_sb[:], COPY, scale=2.0)
+        nc.scalar.activation(rho4[:], rho_sb[:], COPY, scale=4.0)
+
+        w2_grouped = sbuf("w2_grouped", [P, PACK, P * PACK], BF16)
+        w2_codes = sbuf("w2_codes", [P, PACK * P], U32)
+        w2_plane = sbuf("w2_plane", [P, PACK * P], U8)
+
+        rr = sbuf("rr", [P, PACK, S], BF16)
+        for t in range(PACK):
+            source = w1_first[:] if t == 0 else w1_rest[:, t - 1, :]
+            nc.vector.quantize_mx(out=w1_codes[t][:].bitcast(FP8X4), scales=w1_plane[t][:], in_=source)
+            y = psum.tile([P, S], F32, name="y%d" % t)
+            nc.tensor.matmul_mx(
+                out=y[:], lhsT=w1_codes[t][:].bitcast(FP8X4), lhsT_scale=w1_plane[t][:],
+                rhs=x_codes[:].bitcast(FP8X4), rhs_scale=x_plane[:], start=True, stop=True,
+            )
+            t0 = sbuf("t0_%d" % t, [P, S], F32)
+            t0_rho = sbuf("t0_rho%d" % t, [P, S], F32)
+            above = sbuf("above%d" % t, [P, S], F32)
+            clip = sbuf("clip%d" % t, [P, S], F32)
+            halves = [slice(h * HALF, (h + 1) * HALF) for h in range(2)]
+            for cols in halves:
+                nc.vector.scalar_tensor_tensor(t0[:, cols], dual_sb[t][:, cols], 0.5, y[:, cols], ALU.mult, ALU.add)
+                nc.scalar.activation(t0_rho[:, cols], t0[:, cols], COPY, scale=rho2[:, t : t + 1])
+            for cols in halves:
+                nc.vector.tensor_tensor(above[:, cols], t0[:, cols], low_sb[t][:, cols], ALU.max)
+            pieces = halves if t < PACK - 1 else [slice(c, c + CHUNK) for c in range(0, S, CHUNK)]
+            for first in range(0, len(pieces), 2):
+                for cols in pieces[first : first + 2]:
+                    nc.vector.tensor_tensor(clip[:, cols], above[:, cols], high_sb[t][:, cols], ALU.min)
+                for cols in pieces[first : first + 2]:
+                    nc.vector.scalar_tensor_tensor(
+                        rr[:, t, cols], clip[:, cols], rho4[:, t : t + 1], t0_rho[:, cols], ALU.mult, ALU.subtract
+                    )
+            if t == 1:
+                w2_cols = w2_raw[:].rearrange("p j (m t) -> p m j t", t=PACK)
+                w2_dst = w2_grouped[:].rearrange("p t (m j) -> p m j t", j=PACK)
+                step = P // W2_PIECES
+                for m0 in range(0, P, step):
+                    nc.scalar.copy(out=w2_dst[:, m0 : m0 + step], in_=w2_cols[:, m0 : m0 + step])
+            if t == 2:
+                nc.vector.quantize_mx(
+                    out=w2_codes[:].bitcast(FP8X4), scales=w2_plane[:], in_=w2_grouped[:].rearrange("p t w -> p (t w)")
+                )
+
+        out_codes = sbuf("out_codes", [P, S], U32)
+        out_plane = sbuf("out_plane", [P, S], U8)
+        out_words = out_1[0].rearrange("p c t -> p (c t)").bitcast(I32)
+        for c in range(S // CHUNK):
+            cols = slice(c * CHUNK, (c + 1) * CHUNK)
+            rr_grouped = sbuf("rr_grouped%d" % c, [P, CHUNK * PACK], BF16)
+            rr_codes = sbuf("rr_codes%d" % c, [P, CHUNK], U32)
+            rr_plane = sbuf("rr_plane%d" % c, [P, CHUNK], U8)
+            interleave(nc.scalar.copy, rr_grouped[:], rr[:, :, cols])
+            nc.vector.quantize_mx(out=rr_codes[:].bitcast(FP8X4), scales=rr_plane[:], in_=rr_grouped[:])
+            z = psum.tile([P, PACK, CHUNK], F32, name="z%d" % c)
+            for t in range(PACK):
+                rows = slice(t * P, (t + 1) * P)
+                nc.tensor.matmul_mx(
+                    out=z[:, t, :], lhsT=w2_codes[:, rows].bitcast(FP8X4), lhsT_scale=w2_plane[:, rows],
+                    rhs=rr_codes[:].bitcast(FP8X4), rhs_scale=rr_plane[:], start=True, stop=True,
+                )
+            result = sbuf("result%d" % c, [P, PACK, CHUNK], F32)
+            h, inside = divmod(c * CHUNK, HALF)
+            nc.vector.tensor_tensor(result[:], z[:], lin_sb[h][:, :, inside : inside + CHUNK], ALU.add)
+            nc.sync.dma_start(dealt(out_0)[:, :, cols], result[:])
+            out_grouped = sbuf("out_grouped%d" % c, [P, CHUNK * PACK], BF16)
+            interleave(nc.scalar.copy, out_grouped[:], result[:])
+            nc.vector.quantize_mx(out=out_codes[:, cols].bitcast(FP8X4), scales=out_plane[:, cols], in_=out_grouped[:])
+            nc.sync.dma_start(out_words[:, cols], out_codes[:, cols].bitcast(I32))
+        for q in range(QUADS):
+            queue = nc.sync if q % 2 == 0 else nc.scalar
+            queue.dma_start(out_2[0, 4 * q : 4 * q + 4, :].bitcast(I32), out_plane[32 * q : 32 * q + 4, :].bitcast(I32))

@@ -48,25 +48,26 @@ def tile_picked_yosqp_x_po_kernel(
         table_words = sbuf("table_words", [P, T], U32)
         table_scales = sbuf("table_scales", [P, T], U8)
         nc.vector.memset(table_scales[:].bitcast(I32), 0)
+        w1_raw = sbuf("w1_raw", [P, PACK, H], F32)
+        nc.sync.dma_start(w1_raw[:, :2, :], dealt(w1)[:, :2, :])
         nc.sync.dma_start(offsets[:], offs)
-        nc.sync.dma_start(table_words[:].bitcast(I32), x_words[0].rearrange("p c t -> p (c t)").bitcast(I32))
         for q in range(QUADS):
             nc.sync.dma_start(
                 table_scales[32 * q : 32 * q + 4, :].bitcast(I32), x_scales[0, 4 * q : 4 * q + 4, :].bitcast(I32)
             )
-        w1_raw = sbuf("w1_raw", [P, PACK, H], F32)
-        nc.sync.dma_start(w1_raw[:], dealt(w1))
+        nc.sync.dma_start(w1_raw[:, 2:, :], dealt(w1)[:, 2:, :])
+        nc.sync.dma_start(table_words[:].bitcast(I32), x_words[0].rearrange("p c t -> p (c t)").bitcast(I32))
 
-        dual_sb, low_sb, high_sb = [], [], []
         rho_sb = sbuf("rho_sb", [P, PACK], F32)
+        nc.sync.dma_start(rho_sb[:], rho.rearrange("(p t) o -> p (t o)", t=PACK))
         w2_raw = sbuf("w2_raw", [P, PACK, N], F32)
-        for t in range(PACK):
+        parts = [(0, 0, S), (1, 0, HALF), (1, HALF, HALF)]
+        dual_sb, low_sb, high_sb = [], [], []
+        for n, (pair, first, width) in enumerate(parts):
             for name, matrix, tiles in (("dual", dual, dual_sb), ("low", low, low_sb), ("high", high, high_sb)):
-                tiles.append(sbuf("%s%d" % (name, t), [P, S], F32))
-                nc.sync.dma_start(tiles[t][:], dealt(matrix)[:, t, :])
-            if t == 0:
-                nc.sync.dma_start(rho_sb[:], rho.rearrange("(p t) o -> p (t o)", t=PACK))
-            if t == 1:
+                tiles.append(sbuf("%s%d" % (name, n), [P, 2, width], F32))
+                nc.sync.dma_start(tiles[n][:], dealt(matrix)[:, 2 * pair : 2 * pair + 2, first : first + width])
+            if n == 0:
                 nc.sync.dma_start(w2_raw[:], dealt(w2))
         lin_sb = []
         for h in range(2):
@@ -76,15 +77,28 @@ def tile_picked_yosqp_x_po_kernel(
         x_codes = sbuf("x_codes", [P, S], U32)
         x_plane = sbuf("x_plane", [P, S], U8)
         nc.vector.tensor_copy(x_plane[:], table_scales[:].indirect(offsets[:]))
-        nc.vector.tensor_copy(x_codes[:], table_words[:].indirect(offsets[:]))
-
-        w1_first = sbuf("w1_first", [P, P * PACK], BF16)
-        w1_rest = sbuf("w1_rest", [P, PACK - 1, P * PACK], BF16)
         w1_cols = w1_raw[:].rearrange("p j (m t) -> p m j t", t=PACK)
-        nc.vector.tensor_copy(out=w1_first[:].rearrange("p (m j) -> p m j", j=PACK), in_=w1_cols[:, :, :, 0])
-        nc.scalar.copy(out=w1_rest[:].rearrange("p t (m j) -> p m j t", j=PACK), in_=w1_cols[:, :, :, 1:])
-        w1_codes = [sbuf("w1_codes%d" % t, [P, P], U32) for t in range(PACK)]
-        w1_plane = [sbuf("w1_plane%d" % t, [P, P], U8) for t in range(PACK)]
+        w1_grouped = [sbuf("w1_grouped%d" % pair, [P, 2, P * PACK], BF16) for pair in range(2)]
+        w1_codes = [sbuf("w1_codes%d" % pair, [P, 2 * P], U32) for pair in range(2)]
+        w1_plane = [sbuf("w1_plane%d" % pair, [P, 2 * P], U8) for pair in range(2)]
+        for pair, copy in enumerate((nc.vector.tensor_copy, nc.scalar.copy)):
+            copy(
+                out=w1_grouped[pair][:].rearrange("p t (m j) -> p m j t", j=PACK),
+                in_=w1_cols[:, :, :, 2 * pair : 2 * pair + 2],
+            )
+
+        def quantize_w1(pair):
+            nc.vector.quantize_mx(
+                out=w1_codes[pair][:].bitcast(FP8X4),
+                scales=w1_plane[pair][:],
+                in_=w1_grouped[pair][:].rearrange("p t w -> p (t w)"),
+            )
+
+        quantize_w1(0)
+        for h in range(2):
+            entries = offsets[:, h * HALF // 16 : (h + 1) * HALF // 16]
+            nc.vector.tensor_copy(x_codes[:, h * HALF : (h + 1) * HALF], table_words[:].indirect(entries))
+        quantize_w1(1)
 
         rho2 = sbuf("rho2", [P, PACK], F32)
         rho4 = sbuf("rho4", [P, PACK], F32)
@@ -95,53 +109,19 @@ def tile_picked_yosqp_x_po_kernel(
         w2_codes = sbuf("w2_codes", [P, PACK * P], U32)
         w2_plane = sbuf("w2_plane", [P, PACK * P], U8)
 
-        rr = sbuf("rr", [P, PACK, S], BF16)
-        for t in range(PACK):
-            source = w1_first[:] if t == 0 else w1_rest[:, t - 1, :]
-            nc.vector.quantize_mx(out=w1_codes[t][:].bitcast(FP8X4), scales=w1_plane[t][:], in_=source)
-            y = psum.tile([P, S], F32, name="y%d" % t)
-            nc.tensor.matmul_mx(
-                out=y[:], lhsT=w1_codes[t][:].bitcast(FP8X4), lhsT_scale=w1_plane[t][:],
-                rhs=x_codes[:].bitcast(FP8X4), rhs_scale=x_plane[:], start=True, stop=True,
-            )
-            t0 = sbuf("t0_%d" % t, [P, S], F32)
-            t0_rho = sbuf("t0_rho%d" % t, [P, S], F32)
-            above = sbuf("above%d" % t, [P, S], F32)
-            clip = sbuf("clip%d" % t, [P, S], F32)
-            halves = [slice(h * HALF, (h + 1) * HALF) for h in range(2)]
-            for cols in halves:
-                nc.vector.scalar_tensor_tensor(t0[:, cols], dual_sb[t][:, cols], 0.5, y[:, cols], ALU.mult, ALU.add)
-                nc.scalar.activation(t0_rho[:, cols], t0[:, cols], COPY, scale=rho2[:, t : t + 1])
-            for cols in halves:
-                nc.vector.tensor_tensor(above[:, cols], t0[:, cols], low_sb[t][:, cols], ALU.max)
-            pieces = halves if t < PACK - 1 else [slice(c, c + CHUNK) for c in range(0, S, CHUNK)]
-            for first in range(0, len(pieces), 2):
-                for cols in pieces[first : first + 2]:
-                    nc.vector.tensor_tensor(clip[:, cols], above[:, cols], high_sb[t][:, cols], ALU.min)
-                for cols in pieces[first : first + 2]:
-                    nc.vector.scalar_tensor_tensor(
-                        rr[:, t, cols], clip[:, cols], rho4[:, t : t + 1], t0_rho[:, cols], ALU.mult, ALU.subtract
-                    )
-            if t == 1:
-                w2_cols = w2_raw[:].rearrange("p j (m t) -> p m j t", t=PACK)
-                w2_dst = w2_grouped[:].rearrange("p t (m j) -> p m j t", j=PACK)
-                step = P // W2_PIECES
-                for m0 in range(0, P, step):
-                    nc.scalar.copy(out=w2_dst[:, m0 : m0 + step], in_=w2_cols[:, m0 : m0 + step])
-            if t == 2:
-                nc.vector.quantize_mx(
-                    out=w2_codes[:].bitcast(FP8X4), scales=w2_plane[:], in_=w2_grouped[:].rearrange("p t w -> p (t w)")
-                )
-
+        chunks = S // CHUNK
+        rr = sbuf("rr", [P, chunks, PACK, CHUNK], BF16)
         out_codes = sbuf("out_codes", [P, S], U32)
         out_plane = sbuf("out_plane", [P, S], U8)
         out_words = out_1[0].rearrange("p c t -> p (c t)").bitcast(I32)
-        for c in range(S // CHUNK):
+
+        def second_product(c):
             cols = slice(c * CHUNK, (c + 1) * CHUNK)
             rr_grouped = sbuf("rr_grouped%d" % c, [P, CHUNK * PACK], BF16)
             rr_codes = sbuf("rr_codes%d" % c, [P, CHUNK], U32)
             rr_plane = sbuf("rr_plane%d" % c, [P, CHUNK], U8)
-            interleave(nc.scalar.copy, rr_grouped[:], rr[:, :, cols])
+            last = c == chunks - 1
+            interleave(nc.vector.tensor_copy if last else nc.scalar.copy, rr_grouped[:], rr[:, c])
             nc.vector.quantize_mx(out=rr_codes[:].bitcast(FP8X4), scales=rr_plane[:], in_=rr_grouped[:])
             z = psum.tile([P, PACK, CHUNK], F32, name="z%d" % c)
             for t in range(PACK):
@@ -150,14 +130,85 @@ def tile_picked_yosqp_x_po_kernel(
                     out=z[:, t, :], lhsT=w2_codes[:, rows].bitcast(FP8X4), lhsT_scale=w2_plane[:, rows],
                     rhs=rr_codes[:].bitcast(FP8X4), rhs_scale=rr_plane[:], start=True, stop=True,
                 )
+            return z
+
+        def add_and_round(c, z):
+            cols = slice(c * CHUNK, (c + 1) * CHUNK)
+            last = c == chunks - 1
             result = sbuf("result%d" % c, [P, PACK, CHUNK], F32)
             h, inside = divmod(c * CHUNK, HALF)
             nc.vector.tensor_tensor(result[:], z[:], lin_sb[h][:, :, inside : inside + CHUNK], ALU.add)
             nc.sync.dma_start(dealt(out_0)[:, :, cols], result[:])
             out_grouped = sbuf("out_grouped%d" % c, [P, CHUNK * PACK], BF16)
-            interleave(nc.scalar.copy, out_grouped[:], result[:])
+            interleave(nc.vector.tensor_copy if last else nc.scalar.copy, out_grouped[:], result[:])
+            return out_grouped
+
+        def quantize_result(c, out_grouped):
+            cols = slice(c * CHUNK, (c + 1) * CHUNK)
             nc.vector.quantize_mx(out=out_codes[:, cols].bitcast(FP8X4), scales=out_plane[:, cols], in_=out_grouped[:])
             nc.sync.dma_start(out_words[:, cols], out_codes[:, cols].bitcast(I32))
+
+        products = []
+        for n, (pair, first, width) in enumerate(parts):
+            t0 = sbuf("t0_%d" % n, [P, 2, width], F32)
+            t0_rho = sbuf("t0_rho%d" % n, [P, 2, width], F32)
+            above = sbuf("above%d" % n, [P, 2, width], F32)
+            clip = sbuf("clip%d" % n, [P, 2, width], F32)
+            for inside in range(0, width, HALF):
+                cols = slice(first + inside, first + inside + HALF)
+                y = psum.tile([P, 2, HALF], F32, name="y%d_%d" % (n, inside))
+                for u in range(2):
+                    rows = slice(u * P, (u + 1) * P)
+                    nc.tensor.matmul_mx(
+                        out=y[:, u, :], lhsT=w1_codes[pair][:, rows].bitcast(FP8X4), lhsT_scale=w1_plane[pair][:, rows],
+                        rhs=x_codes[:, cols].bitcast(FP8X4), rhs_scale=x_plane[:, cols], start=True, stop=True,
+                    )
+                if pair == 0:
+                    own = slice(inside, inside + HALF)
+                    nc.vector.scalar_tensor_tensor(t0[:, :, own], dual_sb[n][:, :, own], 0.5, y[:], ALU.mult, ALU.add)
+                else:
+                    for u in range(2):
+                        nc.vector.scalar_tensor_tensor(t0[:, u, :], dual_sb[n][:, u, :], 0.5, y[:, u, :], ALU.mult, ALU.add)
+            for u in range(2):
+                t = 2 * pair + u
+                nc.scalar.activation(t0_rho[:, u, :], t0[:, u, :], COPY, scale=rho2[:, t : t + 1])
+            for u in range(2):
+                nc.vector.tensor_tensor(above[:, u, :], t0[:, u, :], low_sb[n][:, u, :], ALU.max)
+            for u in range(2):
+                nc.vector.tensor_tensor(clip[:, u, :], above[:, u, :], high_sb[n][:, u, :], ALU.min)
+            own_chunks = range(first // CHUNK, (first + width) // CHUNK)
+            for u in range(2):
+                t = 2 * pair + u
+                nc.vector.scalar_tensor_tensor(
+                    rr[:, own_chunks.start : own_chunks.stop, t, :],
+                    clip[:, u, :].rearrange("p (c n) -> p c n", n=CHUNK),
+                    rho4[:, t : t + 1],
+                    t0_rho[:, u, :].rearrange("p (c n) -> p c n", n=CHUNK),
+                    ALU.mult,
+                    ALU.subtract,
+                )
+            if n == 0:
+                w2_cols = w2_raw[:].rearrange("p j (m t) -> p m j t", t=PACK)
+                w2_dst = w2_grouped[:].rearrange("p t (m j) -> p m j t", j=PACK)
+                step = P // W2_PIECES
+                for m0 in range(0, P, step):
+                    nc.scalar.copy(out=w2_dst[:, m0 : m0 + step], in_=w2_cols[:, m0 : m0 + step])
+            else:
+                if n == 1:
+                    nc.vector.quantize_mx(
+                        out=w2_codes[:].bitcast(FP8X4),
+                        scales=w2_plane[:],
+                        in_=w2_grouped[:].rearrange("p t w -> p (t w)"),
+                    )
+                for c in own_chunks:
+                    products.append(second_product(c))
+
+        rounded = []
+        for c in range(chunks + 1):
+            if c < chunks:
+                rounded.append(add_and_round(c, products[c]))
+            if c > 0:
+                quantize_result(c - 1, rounded[c - 1])
         for q in range(QUADS):
             queue = nc.sync if q % 2 == 0 else nc.scalar
             queue.dma_start(out_2[0, 4 * q : 4 * q + 4, :].bitcast(I32), out_plane[32 * q : 32 * q + 4, :].bitcast(I32))

@@ -59,7 +59,7 @@ def tile_picked_yosqp_x_po_kernel(
         nc.sync.dma_start(table_words[:].bitcast(I32), x_words[0].rearrange("p c t -> p (c t)").bitcast(I32))
 
         rho_sb = sbuf("rho_sb", [P, PACK], F32)
-        nc.sync.dma_start(rho_sb[:], rho.rearrange("(p t) o -> p (t o)", t=PACK))
+        nc.gpsimd.dma_start(rho_sb[:], rho.rearrange("(p t) o -> p (t o)", t=PACK))
         w2_raw = sbuf("w2_raw", [P, PACK, N], F32)
         parts = [(0, 0, S), (1, 0, HALF), (1, HALF, HALF)]
         dual_sb, low_sb, high_sb = [], [], []
@@ -73,6 +73,11 @@ def tile_picked_yosqp_x_po_kernel(
         for h in range(2):
             lin_sb.append(sbuf("lin%d" % h, [P, PACK, HALF], F32))
             nc.sync.dma_start(lin_sb[h][:], dealt(lin)[:, :, h * HALF : (h + 1) * HALF])
+
+        rho2 = sbuf("rho2", [P, PACK], F32)
+        rho4 = sbuf("rho4", [P, PACK], F32)
+        nc.scalar.activation(rho2[:], rho_sb[:], COPY, scale=2.0)
+        nc.scalar.activation(rho4[:], rho_sb[:], COPY, scale=4.0)
 
         x_codes = sbuf("x_codes", [P, S], U32)
         x_plane = sbuf("x_plane", [P, S], U8)
@@ -100,11 +105,6 @@ def tile_picked_yosqp_x_po_kernel(
             nc.vector.tensor_copy(x_codes[:, h * HALF : (h + 1) * HALF], table_words[:].indirect(entries))
         quantize_w1(1)
 
-        rho2 = sbuf("rho2", [P, PACK], F32)
-        rho4 = sbuf("rho4", [P, PACK], F32)
-        nc.scalar.activation(rho2[:], rho_sb[:], COPY, scale=2.0)
-        nc.scalar.activation(rho4[:], rho_sb[:], COPY, scale=4.0)
-
         w2_grouped = sbuf("w2_grouped", [P, PACK, P * PACK], BF16)
         w2_codes = sbuf("w2_codes", [P, PACK * P], U32)
         w2_plane = sbuf("w2_plane", [P, PACK * P], U8)
@@ -120,8 +120,7 @@ def tile_picked_yosqp_x_po_kernel(
             rr_grouped = sbuf("rr_grouped%d" % c, [P, CHUNK * PACK], BF16)
             rr_codes = sbuf("rr_codes%d" % c, [P, CHUNK], U32)
             rr_plane = sbuf("rr_plane%d" % c, [P, CHUNK], U8)
-            last = c == chunks - 1
-            interleave(nc.vector.tensor_copy if last else nc.scalar.copy, rr_grouped[:], rr[:, c])
+            interleave(nc.scalar.copy, rr_grouped[:], rr[:, c])
             nc.vector.quantize_mx(out=rr_codes[:].bitcast(FP8X4), scales=rr_plane[:], in_=rr_grouped[:])
             z = psum.tile([P, PACK, CHUNK], F32, name="z%d" % c)
             for t in range(PACK):
@@ -134,7 +133,7 @@ def tile_picked_yosqp_x_po_kernel(
 
         def add_and_round(c, z):
             cols = slice(c * CHUNK, (c + 1) * CHUNK)
-            last = c == chunks - 1
+            last = c % 2 == 1
             result = sbuf("result%d" % c, [P, PACK, CHUNK], F32)
             h, inside = divmod(c * CHUNK, HALF)
             nc.vector.tensor_tensor(result[:], z[:], lin_sb[h][:, :, inside : inside + CHUNK], ALU.add)
@@ -172,21 +171,28 @@ def tile_picked_yosqp_x_po_kernel(
             for u in range(2):
                 t = 2 * pair + u
                 nc.scalar.activation(t0_rho[:, u, :], t0[:, u, :], COPY, scale=rho2[:, t : t + 1])
-            for u in range(2):
-                nc.vector.tensor_tensor(above[:, u, :], t0[:, u, :], low_sb[n][:, u, :], ALU.max)
-            for u in range(2):
-                nc.vector.tensor_tensor(clip[:, u, :], above[:, u, :], high_sb[n][:, u, :], ALU.min)
+            if pair == 0:
+                pieces = [(slice(0, 2), slice(inside, inside + HALF)) for inside in range(0, width, HALF)]
+            else:
+                pieces = [(slice(u, u + 1), slice(0, width)) for u in range(2)]
+            for slots, own in pieces:
+                nc.vector.tensor_tensor(above[:, slots, own], t0[:, slots, own], low_sb[n][:, slots, own], ALU.max)
+            for slots, own in pieces:
+                nc.vector.tensor_tensor(clip[:, slots, own], above[:, slots, own], high_sb[n][:, slots, own], ALU.min)
             own_chunks = range(first // CHUNK, (first + width) // CHUNK)
-            for u in range(2):
-                t = 2 * pair + u
-                nc.vector.scalar_tensor_tensor(
-                    rr[:, own_chunks.start : own_chunks.stop, t, :],
-                    clip[:, u, :].rearrange("p (c n) -> p c n", n=CHUNK),
-                    rho4[:, t : t + 1],
-                    t0_rho[:, u, :].rearrange("p (c n) -> p c n", n=CHUNK),
-                    ALU.mult,
-                    ALU.subtract,
-                )
+            run = CHUNK if n == len(parts) - 1 else HALF
+            for inside in range(0, width, run):
+                for u in range(2):
+                    t = 2 * pair + u
+                    c0 = (first + inside) // CHUNK
+                    nc.vector.scalar_tensor_tensor(
+                        rr[:, c0 : c0 + run // CHUNK, t, :],
+                        clip[:, u, inside : inside + run].rearrange("p (c n) -> p c n", n=CHUNK),
+                        rho4[:, t : t + 1],
+                        t0_rho[:, u, inside : inside + run].rearrange("p (c n) -> p c n", n=CHUNK),
+                        ALU.mult,
+                        ALU.subtract,
+                    )
             if n == 0:
                 w2_cols = w2_raw[:].rearrange("p j (m t) -> p m j t", t=PACK)
                 w2_dst = w2_grouped[:].rearrange("p t (m j) -> p m j t", j=PACK)

@@ -16,10 +16,12 @@ ALU = mybir.AluOpType
 COPY = mybir.ActivationFunctionType.Copy
 
 P = 128
-PACK = 4
-QUADS = 4
+SLOTS = 4
+QUADRANTS = 4
+LIST_ROWS = 16
 HALF = S // 2
 CHUNK = 128
+CHUNKS = S // CHUNK
 RUN = 4
 W2_PIECES = 4
 
@@ -36,185 +38,186 @@ def tile_picked_yosqp_x_po_kernel(
             return held.tile(shape, dtype, name=name, align_bytes=64)
 
         def dealt(matrix):
-            return matrix.rearrange("(p t) c -> p t c", t=PACK)
+            return matrix.rearrange("(p t) c -> p t c", t=SLOTS)
 
-        def interleave(copy, dst, src):
+        def load(name, source):
+            tile = sbuf(name, list(source.shape), F32)
+            nc.sync.dma_start(tile[:], source)
+            return tile
+
+        def interleave(copy, grouped, slots):
             copy(
-                out=dst.rearrange("p (c i t) -> p c t i", i=RUN, t=PACK),
-                in_=src.rearrange("p t (c i) -> p c t i", i=RUN),
+                out=grouped.rearrange("p (c i t) -> p c t i", i=RUN, t=SLOTS),
+                in_=slots.rearrange("p t (c i) -> p c t i", i=RUN),
             )
 
-        offsets = held.tile([P, S // 16], U16, name="offsets")
+        def quantize(codes, plane, grouped):
+            nc.vector.quantize_mx(out=codes.bitcast(FP8X4), scales=plane, in_=grouped)
+
+        def multiply(out, w_codes, w_plane, codes, plane):
+            nc.tensor.matmul_mx(
+                out=out,
+                lhsT=w_codes.bitcast(FP8X4),
+                lhsT_scale=w_plane,
+                rhs=codes.bitcast(FP8X4),
+                rhs_scale=plane,
+                start=True,
+                stop=True,
+            )
+
+        pair_slots = [slice(0, 2), slice(2, 4)]
+        halves = [slice(h * HALF, (h + 1) * HALF) for h in range(2)]
+
+        offsets = held.tile([P, S // LIST_ROWS], U16, name="offsets")
         table_words = sbuf("table_words", [P, T], U32)
         table_scales = sbuf("table_scales", [P, T], U8)
         nc.vector.memset(table_scales[:].bitcast(I32), 0)
-        w1_raw = sbuf("w1_raw", [P, PACK, H], F32)
-        nc.sync.dma_start(w1_raw[:, :2, :], dealt(w1)[:, :2, :])
+        w1_raw = sbuf("w1_raw", [P, SLOTS, H], F32)
+        nc.sync.dma_start(w1_raw[:, pair_slots[0], :], dealt(w1)[:, pair_slots[0], :])
         nc.sync.dma_start(offsets[:], offs)
-        for q in range(QUADS):
+        for q in range(QUADRANTS):
             nc.sync.dma_start(
                 table_scales[32 * q : 32 * q + 4, :].bitcast(I32), x_scales[0, 4 * q : 4 * q + 4, :].bitcast(I32)
             )
-        nc.sync.dma_start(w1_raw[:, 2:, :], dealt(w1)[:, 2:, :])
+        nc.sync.dma_start(w1_raw[:, pair_slots[1], :], dealt(w1)[:, pair_slots[1], :])
         nc.sync.dma_start(table_words[:].bitcast(I32), x_words[0].rearrange("p c t -> p (c t)").bitcast(I32))
+        rho_sb = sbuf("rho_sb", [P, SLOTS], F32)
+        nc.gpsimd.dma_start(rho_sb[:], rho.rearrange("(p t) o -> p (t o)", t=SLOTS))
+        def load_part(name, pair, cols):
+            return [
+                load("%s_%s" % (kind, name), dealt(matrix)[:, pair_slots[pair], cols])
+                for kind, matrix in (("dual", dual), ("low", low), ("high", high))
+            ]
 
-        rho_sb = sbuf("rho_sb", [P, PACK], F32)
-        nc.gpsimd.dma_start(rho_sb[:], rho.rearrange("(p t) o -> p (t o)", t=PACK))
-        w2_raw = sbuf("w2_raw", [P, PACK, N], F32)
-        parts = [(0, 0, S), (1, 0, HALF), (1, HALF, HALF)]
-        dual_sb, low_sb, high_sb = [], [], []
-        for n, (pair, first, width) in enumerate(parts):
-            for name, matrix, tiles in (("dual", dual, dual_sb), ("low", low, low_sb), ("high", high, high_sb)):
-                tiles.append(sbuf("%s%d" % (name, n), [P, 2, width], F32))
-                nc.sync.dma_start(tiles[n][:], dealt(matrix)[:, 2 * pair : 2 * pair + 2, first : first + width])
-            if n == 0:
-                nc.sync.dma_start(w2_raw[:], dealt(w2))
-        lin_sb = []
-        for h in range(2):
-            lin_sb.append(sbuf("lin%d" % h, [P, PACK, HALF], F32))
-            nc.sync.dma_start(lin_sb[h][:], dealt(lin)[:, :, h * HALF : (h + 1) * HALF])
+        part_whole = load_part("whole", 0, slice(0, S))
+        w2_raw = load("w2_raw", dealt(w2))
+        part_half = [load_part("half%d" % h, 1, halves[h]) for h in range(2)]
+        lin_sb = [load("lin%d" % h, dealt(lin)[:, :, halves[h]]) for h in range(2)]
 
-        rho2 = sbuf("rho2", [P, PACK], F32)
-        rho4 = sbuf("rho4", [P, PACK], F32)
+        rho2 = sbuf("rho2", [P, SLOTS], F32)
+        rho4 = sbuf("rho4", [P, SLOTS], F32)
         nc.scalar.activation(rho2[:], rho_sb[:], COPY, scale=2.0)
         nc.scalar.activation(rho4[:], rho_sb[:], COPY, scale=4.0)
 
         x_codes = sbuf("x_codes", [P, S], U32)
         x_plane = sbuf("x_plane", [P, S], U8)
         nc.vector.tensor_copy(x_plane[:], table_scales[:].indirect(offsets[:]))
-        w1_cols = w1_raw[:].rearrange("p j (m t) -> p m j t", t=PACK)
-        w1_grouped = [sbuf("w1_grouped%d" % pair, [P, 2, P * PACK], BF16) for pair in range(2)]
+        w1_cols = w1_raw[:].rearrange("p j (m t) -> p m j t", t=SLOTS)
+        w1_grouped = [sbuf("w1_grouped%d" % pair, [P, 2, P * SLOTS], BF16) for pair in range(2)]
         w1_codes = [sbuf("w1_codes%d" % pair, [P, 2 * P], U32) for pair in range(2)]
         w1_plane = [sbuf("w1_plane%d" % pair, [P, 2 * P], U8) for pair in range(2)]
         for pair, copy in enumerate((nc.vector.tensor_copy, nc.scalar.copy)):
             copy(
-                out=w1_grouped[pair][:].rearrange("p t (m j) -> p m j t", j=PACK),
-                in_=w1_cols[:, :, :, 2 * pair : 2 * pair + 2],
+                out=w1_grouped[pair][:].rearrange("p u (m j) -> p m j u", j=SLOTS),
+                in_=w1_cols[:, :, :, pair_slots[pair]],
             )
+        quantize(w1_codes[0][:], w1_plane[0][:], w1_grouped[0][:].rearrange("p u w -> p (u w)"))
+        for cols in halves:
+            entries = offsets[:, cols.start // LIST_ROWS : cols.stop // LIST_ROWS]
+            nc.vector.tensor_copy(x_codes[:, cols], table_words[:].indirect(entries))
+        quantize(w1_codes[1][:], w1_plane[1][:], w1_grouped[1][:].rearrange("p u w -> p (u w)"))
 
-        def quantize_w1(pair):
-            nc.vector.quantize_mx(
-                out=w1_codes[pair][:].bitcast(FP8X4),
-                scales=w1_plane[pair][:],
-                in_=w1_grouped[pair][:].rearrange("p t w -> p (t w)"),
-            )
+        rr = sbuf("rr", [P, CHUNKS, SLOTS, CHUNK], BF16)
 
-        quantize_w1(0)
-        for h in range(2):
-            entries = offsets[:, h * HALF // 16 : (h + 1) * HALF // 16]
-            nc.vector.tensor_copy(x_codes[:, h * HALF : (h + 1) * HALF], table_words[:].indirect(entries))
-        quantize_w1(1)
+        def first_stage(pair, first, part, pieces, step):
+            dual_sb, low_sb, high_sb = part
+            width = dual_sb.shape[2]
+            t0, t0_rho, above, clip = [
+                sbuf("%s%d_%d" % (kind, pair, first), [P, 2, width], F32) for kind in ("t0_", "t0_rho", "above", "clip")
+            ]
+            for inside in range(0, width, HALF):
+                y = psum.tile([P, 2, HALF], F32, name="y%d_%d" % (pair, first + inside))
+                tokens = slice(first + inside, first + inside + HALF)
+                for u in range(2):
+                    rows = slice(u * P, (u + 1) * P)
+                    multiply(
+                        y[:, u, :], w1_codes[pair][:, rows], w1_plane[pair][:, rows], x_codes[:, tokens], x_plane[:, tokens]
+                    )
+                for slots, cols in pieces:
+                    if cols.start == inside:
+                        nc.vector.scalar_tensor_tensor(
+                            t0[:, slots, cols], dual_sb[:, slots, cols], 0.5, y[:, slots, :], ALU.mult, ALU.add
+                        )
+            for u in range(2):
+                t = 2 * pair + u
+                nc.scalar.activation(t0_rho[:, u, :], t0[:, u, :], COPY, scale=rho2[:, t : t + 1])
+            for slots, cols in pieces:
+                nc.vector.tensor_tensor(above[:, slots, cols], t0[:, slots, cols], low_sb[:, slots, cols], ALU.max)
+            for slots, cols in pieces:
+                nc.vector.tensor_tensor(clip[:, slots, cols], above[:, slots, cols], high_sb[:, slots, cols], ALU.min)
+            for inside in range(0, width, step):
+                start = first + inside
+                for u in range(2):
+                    t = 2 * pair + u
+                    nc.vector.scalar_tensor_tensor(
+                        rr[:, start // CHUNK : (start + step) // CHUNK, t, :],
+                        clip[:, u, inside : inside + step].rearrange("p (c n) -> p c n", n=CHUNK),
+                        rho4[:, t : t + 1],
+                        t0_rho[:, u, inside : inside + step].rearrange("p (c n) -> p c n", n=CHUNK),
+                        ALU.mult,
+                        ALU.subtract,
+                    )
 
-        w2_grouped = sbuf("w2_grouped", [P, PACK, P * PACK], BF16)
-        w2_codes = sbuf("w2_codes", [P, PACK * P], U32)
-        w2_plane = sbuf("w2_plane", [P, PACK * P], U8)
+        w2_codes = sbuf("w2_codes", [P, SLOTS * P], U32)
+        w2_plane = sbuf("w2_plane", [P, SLOTS * P], U8)
 
-        chunks = S // CHUNK
-        rr = sbuf("rr", [P, chunks, PACK, CHUNK], BF16)
+        def second_product(c):
+            rr_grouped = sbuf("rr_grouped%d" % c, [P, CHUNK * SLOTS], BF16)
+            rr_codes = sbuf("rr_codes%d" % c, [P, CHUNK], U32)
+            rr_plane = sbuf("rr_plane%d" % c, [P, CHUNK], U8)
+            interleave(nc.scalar.copy, rr_grouped[:], rr[:, c])
+            quantize(rr_codes[:], rr_plane[:], rr_grouped[:])
+            z = psum.tile([P, SLOTS, CHUNK], F32, name="z%d" % c)
+            for t in range(SLOTS):
+                rows = slice(t * P, (t + 1) * P)
+                multiply(z[:, t, :], w2_codes[:, rows], w2_plane[:, rows], rr_codes[:], rr_plane[:])
+            return z
+
+        by_columns = [(slice(0, 2), cols) for cols in halves]
+        by_slots = [(slice(u, u + 1), slice(0, HALF)) for u in range(2)]
+        first_stage(0, 0, part_whole, by_columns, HALF)
+
+        w2_grouped = sbuf("w2_grouped", [P, SLOTS, P * SLOTS], BF16)
+        w2_cols = w2_raw[:].rearrange("p j (m t) -> p m j t", t=SLOTS)
+        w2_dealt = w2_grouped[:].rearrange("p t (m j) -> p m j t", j=SLOTS)
+        piece = P // W2_PIECES
+        for m in range(0, P, piece):
+            nc.scalar.copy(out=w2_dealt[:, m : m + piece], in_=w2_cols[:, m : m + piece])
+
+        products = []
+        first_stage(1, 0, part_half[0], by_slots, HALF)
+        quantize(w2_codes[:], w2_plane[:], w2_grouped[:].rearrange("p t w -> p (t w)"))
+        products.extend([second_product(c) for c in range(CHUNKS // 2)])
+        first_stage(1, HALF, part_half[1], by_slots, CHUNK)
+        products.extend([second_product(c) for c in range(CHUNKS // 2, CHUNKS)])
+
         out_codes = sbuf("out_codes", [P, S], U32)
         out_plane = sbuf("out_plane", [P, S], U8)
         out_words = out_1[0].rearrange("p c t -> p (c t)").bitcast(I32)
 
-        def second_product(c):
+        def add_and_round(c):
             cols = slice(c * CHUNK, (c + 1) * CHUNK)
-            rr_grouped = sbuf("rr_grouped%d" % c, [P, CHUNK * PACK], BF16)
-            rr_codes = sbuf("rr_codes%d" % c, [P, CHUNK], U32)
-            rr_plane = sbuf("rr_plane%d" % c, [P, CHUNK], U8)
-            interleave(nc.scalar.copy, rr_grouped[:], rr[:, c])
-            nc.vector.quantize_mx(out=rr_codes[:].bitcast(FP8X4), scales=rr_plane[:], in_=rr_grouped[:])
-            z = psum.tile([P, PACK, CHUNK], F32, name="z%d" % c)
-            for t in range(PACK):
-                rows = slice(t * P, (t + 1) * P)
-                nc.tensor.matmul_mx(
-                    out=z[:, t, :], lhsT=w2_codes[:, rows].bitcast(FP8X4), lhsT_scale=w2_plane[:, rows],
-                    rhs=rr_codes[:].bitcast(FP8X4), rhs_scale=rr_plane[:], start=True, stop=True,
-                )
-            return z
-
-        def add_and_round(c, z):
-            cols = slice(c * CHUNK, (c + 1) * CHUNK)
-            last = c % 2 == 1
-            result = sbuf("result%d" % c, [P, PACK, CHUNK], F32)
-            h, inside = divmod(c * CHUNK, HALF)
-            nc.vector.tensor_tensor(result[:], z[:], lin_sb[h][:, :, inside : inside + CHUNK], ALU.add)
+            h, inside = divmod(cols.start, HALF)
+            result = sbuf("result%d" % c, [P, SLOTS, CHUNK], F32)
+            nc.vector.tensor_tensor(result[:], products[c][:], lin_sb[h][:, :, inside : inside + CHUNK], ALU.add)
             nc.sync.dma_start(dealt(out_0)[:, :, cols], result[:])
-            out_grouped = sbuf("out_grouped%d" % c, [P, CHUNK * PACK], BF16)
-            interleave(nc.vector.tensor_copy if last else nc.scalar.copy, out_grouped[:], result[:])
+            out_grouped = sbuf("out_grouped%d" % c, [P, CHUNK * SLOTS], BF16)
+            interleave(nc.scalar.copy if c % 2 == 0 else nc.vector.tensor_copy, out_grouped[:], result[:])
             return out_grouped
 
         def quantize_result(c, out_grouped):
             cols = slice(c * CHUNK, (c + 1) * CHUNK)
-            nc.vector.quantize_mx(out=out_codes[:, cols].bitcast(FP8X4), scales=out_plane[:, cols], in_=out_grouped[:])
-            nc.sync.dma_start(out_words[:, cols], out_codes[:, cols].bitcast(I32))
-
-        products = []
-        for n, (pair, first, width) in enumerate(parts):
-            t0 = sbuf("t0_%d" % n, [P, 2, width], F32)
-            t0_rho = sbuf("t0_rho%d" % n, [P, 2, width], F32)
-            above = sbuf("above%d" % n, [P, 2, width], F32)
-            clip = sbuf("clip%d" % n, [P, 2, width], F32)
-            for inside in range(0, width, HALF):
-                cols = slice(first + inside, first + inside + HALF)
-                y = psum.tile([P, 2, HALF], F32, name="y%d_%d" % (n, inside))
-                for u in range(2):
-                    rows = slice(u * P, (u + 1) * P)
-                    nc.tensor.matmul_mx(
-                        out=y[:, u, :], lhsT=w1_codes[pair][:, rows].bitcast(FP8X4), lhsT_scale=w1_plane[pair][:, rows],
-                        rhs=x_codes[:, cols].bitcast(FP8X4), rhs_scale=x_plane[:, cols], start=True, stop=True,
-                    )
-                if pair == 0:
-                    own = slice(inside, inside + HALF)
-                    nc.vector.scalar_tensor_tensor(t0[:, :, own], dual_sb[n][:, :, own], 0.5, y[:], ALU.mult, ALU.add)
-                else:
-                    for u in range(2):
-                        nc.vector.scalar_tensor_tensor(t0[:, u, :], dual_sb[n][:, u, :], 0.5, y[:, u, :], ALU.mult, ALU.add)
-            for u in range(2):
-                t = 2 * pair + u
-                nc.scalar.activation(t0_rho[:, u, :], t0[:, u, :], COPY, scale=rho2[:, t : t + 1])
-            if pair == 0:
-                pieces = [(slice(0, 2), slice(inside, inside + HALF)) for inside in range(0, width, HALF)]
-            else:
-                pieces = [(slice(u, u + 1), slice(0, width)) for u in range(2)]
-            for slots, own in pieces:
-                nc.vector.tensor_tensor(above[:, slots, own], t0[:, slots, own], low_sb[n][:, slots, own], ALU.max)
-            for slots, own in pieces:
-                nc.vector.tensor_tensor(clip[:, slots, own], above[:, slots, own], high_sb[n][:, slots, own], ALU.min)
-            own_chunks = range(first // CHUNK, (first + width) // CHUNK)
-            run = CHUNK if n == len(parts) - 1 else HALF
-            for inside in range(0, width, run):
-                for u in range(2):
-                    t = 2 * pair + u
-                    c0 = (first + inside) // CHUNK
-                    nc.vector.scalar_tensor_tensor(
-                        rr[:, c0 : c0 + run // CHUNK, t, :],
-                        clip[:, u, inside : inside + run].rearrange("p (c n) -> p c n", n=CHUNK),
-                        rho4[:, t : t + 1],
-                        t0_rho[:, u, inside : inside + run].rearrange("p (c n) -> p c n", n=CHUNK),
-                        ALU.mult,
-                        ALU.subtract,
-                    )
-            if n == 0:
-                w2_cols = w2_raw[:].rearrange("p j (m t) -> p m j t", t=PACK)
-                w2_dst = w2_grouped[:].rearrange("p t (m j) -> p m j t", j=PACK)
-                step = P // W2_PIECES
-                for m0 in range(0, P, step):
-                    nc.scalar.copy(out=w2_dst[:, m0 : m0 + step], in_=w2_cols[:, m0 : m0 + step])
-            else:
-                if n == 1:
-                    nc.vector.quantize_mx(
-                        out=w2_codes[:].bitcast(FP8X4),
-                        scales=w2_plane[:],
-                        in_=w2_grouped[:].rearrange("p t w -> p (t w)"),
-                    )
-                for c in own_chunks:
-                    products.append(second_product(c))
+            quantize(out_codes[:, cols], out_plane[:, cols], out_grouped[:])
+            if c % 2 == 1:
+                half = halves[c // 2]
+                nc.sync.dma_start(out_words[:, half], out_codes[:, half].bitcast(I32))
 
         rounded = []
-        for c in range(chunks + 1):
-            if c < chunks:
-                rounded.append(add_and_round(c, products[c]))
+        for c in range(CHUNKS):
+            rounded.append(add_and_round(c))
             if c > 0:
                 quantize_result(c - 1, rounded[c - 1])
-        for q in range(QUADS):
+        quantize_result(CHUNKS - 1, rounded[-1])
+        for q in range(QUADRANTS):
             queue = nc.sync if q % 2 == 0 else nc.scalar
             queue.dma_start(out_2[0, 4 * q : 4 * q + 4, :].bitcast(I32), out_plane[32 * q : 32 * q + 4, :].bitcast(I32))

from contextlib import ExitStack

import concourse.mybir as mybir

K, T, S, H, N = 512, 1024, 512, 512, 512
FLOPS = 2 * K * H * S + 2 * H * N * S

F32 = mybir.dt.float32
BF16 = mybir.dt.bfloat16
I32 = mybir.dt.int32
U32 = mybir.dt.uint32
U16 = mybir.dt.uint16
U8 = mybir.dt.uint8
FP8X4 = mybir.dt.float8_e4m3fn_x4
ALU = mybir.AluOpType
COPY = mybir.ActivationFunctionType.Copy

P = 128
SLOTS = 4
QUADRANTS = 4
LIST_ROWS = 16
HALF = S // 2
CHUNK = 128
CHUNKS = S // CHUNK
RUN = 4
W2_PIECES = 4


def tile_picked_yosqp_x_po_kernel(
    tc, x_words, x_scales, w1, dual, low, high, rho, w2, lin, offs, out_0, out_1, out_2
):
    nc = tc.nc
    with ExitStack() as ctx:
        held = ctx.enter_context(tc.tile_pool(name="held", bufs=1))
        psum = ctx.enter_context(tc.psum_pool(name="psum", bufs=1))

        def sbuf(name, shape, dtype):
            return held.tile(shape, dtype, name=name, align_bytes=64)

        def dealt(matrix):
            return matrix.rearrange("(p t) c -> p t c", t=SLOTS)

        def load(name, source):
            tile = sbuf(name, list(source.shape), F32)
            nc.sync.dma_start(tile[:], source)
            return tile

        def interleave(copy, grouped, slots):
            copy(
                out=grouped.rearrange("p (c i t) -> p c t i", i=RUN, t=SLOTS),
                in_=slots.rearrange("p t (c i) -> p c t i", i=RUN),
            )

        def quantize(codes, plane, grouped):
            nc.vector.quantize_mx(out=codes.bitcast(FP8X4), scales=plane, in_=grouped)

        def multiply(out, w_codes, w_plane, codes, plane):
            nc.tensor.matmul_mx(
                out=out,
                lhsT=w_codes.bitcast(FP8X4),
                lhsT_scale=w_plane,
                rhs=codes.bitcast(FP8X4),
                rhs_scale=plane,
                start=True,
                stop=True,
            )

        pair_slots = [slice(0, 2), slice(2, 4)]
        halves = [slice(h * HALF, (h + 1) * HALF) for h in range(2)]

        offsets = held.tile([P, S // LIST_ROWS], U16, name="offsets")
        table_words = sbuf("table_words", [P, T], U32)
        table_scales = sbuf("table_scales", [P, T], U8)
        nc.vector.memset(table_scales[:].bitcast(I32), 0)
        w1_raw = sbuf("w1_raw", [P, SLOTS, H], F32)
        nc.sync.dma_start(w1_raw[:, pair_slots[0], :], dealt(w1)[:, pair_slots[0], :])
        nc.sync.dma_start(offsets[:], offs)
        for q in range(QUADRANTS):
            nc.sync.dma_start(
                table_scales[32 * q : 32 * q + 4, :].bitcast(I32), x_scales[0, 4 * q : 4 * q + 4, :].bitcast(I32)
            )
        nc.sync.dma_start(w1_raw[:, pair_slots[1], :], dealt(w1)[:, pair_slots[1], :])
        nc.sync.dma_start(table_words[:].bitcast(I32), x_words[0].rearrange("p c t -> p (c t)").bitcast(I32))
        rho_sb = sbuf("rho_sb", [P, SLOTS], F32)
        nc.gpsimd.dma_start(rho_sb[:], rho.rearrange("(p t) o -> p (t o)", t=SLOTS))
        def load_part(name, pair, cols):
            return [
                load("%s_%s" % (kind, name), dealt(matrix)[:, pair_slots[pair], cols])
                for kind, matrix in (("dual", dual), ("low", low), ("high", high))
            ]

        part_whole = load_part("whole", 0, slice(0, S))
        w2_raw = load("w2_raw", dealt(w2))
        part_half = [load_part("half%d" % h, 1, halves[h]) for h in range(2)]
        lin_sb = [load("lin%d" % h, dealt(lin)[:, :, halves[h]]) for h in range(2)]

        rho2 = sbuf("rho2", [P, SLOTS], F32)
        rho4 = sbuf("rho4", [P, SLOTS], F32)
        nc.scalar.activation(rho2[:], rho_sb[:], COPY, scale=2.0)
        nc.scalar.activation(rho4[:], rho_sb[:], COPY, scale=4.0)

        x_codes = sbuf("x_codes", [P, S], U32)
        x_plane = sbuf("x_plane", [P, S], U8)
        nc.vector.tensor_copy(x_plane[:], table_scales[:].indirect(offsets[:]))
        w1_cols = w1_raw[:].rearrange("p j (m t) -> p m j t", t=SLOTS)
        w1_grouped = [sbuf("w1_grouped%d" % pair, [P, 2, P * SLOTS], BF16) for pair in range(2)]
        w1_codes = [sbuf("w1_codes%d" % pair, [P, 2 * P], U32) for pair in range(2)]
        w1_plane = [sbuf("w1_plane%d" % pair, [P, 2 * P], U8) for pair in range(2)]
        for pair, copy in enumerate((nc.vector.tensor_copy, nc.scalar.copy)):
            copy(
                out=w1_grouped[pair][:].rearrange("p u (m j) -> p m j u", j=SLOTS),
                in_=w1_cols[:, :, :, pair_slots[pair]],
            )
        quantize(w1_codes[0][:], w1_plane[0][:], w1_grouped[0][:].rearrange("p u w -> p (u w)"))
        for cols in halves:
            entries = offsets[:, cols.start // LIST_ROWS : cols.stop // LIST_ROWS]
            nc.vector.tensor_copy(x_codes[:, cols], table_words[:].indirect(entries))
        quantize(w1_codes[1][:], w1_plane[1][:], w1_grouped[1][:].rearrange("p u w -> p (u w)"))

        rr = sbuf("rr", [P, CHUNKS, SLOTS, CHUNK], BF16)

        def first_stage(pair, first, part, pieces, step):
            dual_sb, low_sb, high_sb = part
            width = dual_sb.shape[2]
            t0, t0_rho, above, clip = [
                sbuf("%s%d_%d" % (kind, pair, first), [P, 2, width], F32) for kind in ("t0_", "t0_rho", "above", "clip")
            ]
            for inside in range(0, width, HALF):
                y = psum.tile([P, 2, HALF], F32, name="y%d_%d" % (pair, first + inside))
                tokens = slice(first + inside, first + inside + HALF)
                for u in range(2):
                    rows = slice(u * P, (u + 1) * P)
                    multiply(
                        y[:, u, :], w1_codes[pair][:, rows], w1_plane[pair][:, rows], x_codes[:, tokens], x_plane[:, tokens]
                    )
                for slots, cols in pieces:
                    if cols.start == inside:
                        nc.vector.scalar_tensor_tensor(
                            t0[:, slots, cols], dual_sb[:, slots, cols], 0.5, y[:, slots, :], ALU.mult, ALU.add
                        )
            for u in range(2):
                t = 2 * pair + u
                nc.scalar.activation(t0_rho[:, u, :], t0[:, u, :], COPY, scale=rho2[:, t : t + 1])
            for slots, cols in pieces:
                nc.vector.tensor_tensor(above[:, slots, cols], t0[:, slots, cols], low_sb[:, slots, cols], ALU.max)
            for slots, cols in pieces:
                nc.vector.tensor_tensor(clip[:, slots, cols], above[:, slots, cols], high_sb[:, slots, cols], ALU.min)
            for inside in range(0, width, step):
                start = first + inside
                for u in range(2):
                    t = 2 * pair + u
                    nc.vector.scalar_tensor_tensor(
                        rr[:, start // CHUNK : (start + step) // CHUNK, t, :],
                        clip[:, u, inside : inside + step].rearrange("p (c n) -> p c n", n=CHUNK),
                        rho4[:, t : t + 1],
                        t0_rho[:, u, inside : inside + step].rearrange("p (c n) -> p c n", n=CHUNK),
                        ALU.mult,
                        ALU.subtract,
                    )

        w2_codes = sbuf("w2_codes", [P, SLOTS * P], U32)
        w2_plane = sbuf("w2_plane", [P, SLOTS * P], U8)

        def second_product(c):
            rr_grouped = sbuf("rr_grouped%d" % c, [P, CHUNK * SLOTS], BF16)
            rr_codes = sbuf("rr_codes%d" % c, [P, CHUNK], U32)
            rr_plane = sbuf("rr_plane%d" % c, [P, CHUNK], U8)
            interleave(nc.scalar.copy, rr_grouped[:], rr[:, c])
            quantize(rr_codes[:], rr_plane[:], rr_grouped[:])
            z = psum.tile([P, SLOTS, CHUNK], F32, name="z%d" % c)
            for t in range(SLOTS):
                rows = slice(t * P, (t + 1) * P)
                multiply(z[:, t, :], w2_codes[:, rows], w2_plane[:, rows], rr_codes[:], rr_plane[:])
            return z

        by_columns = [(slice(0, 2), cols) for cols in halves]
        by_slots = [(slice(u, u + 1), slice(0, HALF)) for u in range(2)]
        first_stage(0, 0, part_whole, by_columns, HALF)

        w2_grouped = sbuf("w2_grouped", [P, SLOTS, P * SLOTS], BF16)
        w2_cols = w2_raw[:].rearrange("p j (m t) -> p m j t", t=SLOTS)
        w2_dealt = w2_grouped[:].rearrange("p t (m j) -> p m j t", j=SLOTS)
        piece = P // W2_PIECES
        for m in range(0, P, piece):
            nc.scalar.copy(out=w2_dealt[:, m : m + piece], in_=w2_cols[:, m : m + piece])

        products = []
        first_stage(1, 0, part_half[0], by_slots, HALF)
        quantize(w2_codes[:], w2_plane[:], w2_grouped[:].rearrange("p t w -> p (t w)"))
        products.extend([second_product(c) for c in range(CHUNKS // 2)])
        first_stage(1, HALF, part_half[1], by_slots, CHUNK)
        products.extend([second_product(c) for c in range(CHUNKS // 2, CHUNKS)])

        out_codes = sbuf("out_codes", [P, S], U32)
        out_plane = sbuf("out_plane", [P, S], U8)
        out_words = out_1[0].rearrange("p c t -> p (c t)").bitcast(I32)

        def add_and_round(c):
            cols = slice(c * CHUNK, (c + 1) * CHUNK)
            h, inside = divmod(cols.start, HALF)
            result = sbuf("result%d" % c, [P, SLOTS, CHUNK], F32)
            nc.vector.tensor_tensor(result[:], products[c][:], lin_sb[h][:, :, inside : inside + CHUNK], ALU.add)
            nc.sync.dma_start(dealt(out_0)[:, :, cols], result[:])
            out_grouped = sbuf("out_grouped%d" % c, [P, CHUNK * SLOTS], BF16)
            interleave(nc.scalar.copy if c % 2 == 0 else nc.vector.tensor_copy, out_grouped[:], result[:])
            return out_grouped

        def quantize_result(c, out_grouped):
            cols = slice(c * CHUNK, (c + 1) * CHUNK)
            quantize(out_codes[:, cols], out_plane[:, cols], out_grouped[:])
            if c % 2 == 1:
                half = halves[c // 2]
                nc.sync.dma_start(out_words[:, half], out_codes[:, half].bitcast(I32))

        rounded = []
        for c in range(CHUNKS):
            rounded.append(add_and_round(c))
            if c > 0:
                quantize_result(c - 1, rounded[c - 1])
        quantize_result(CHUNKS - 1, rounded[-1])
        for q in range(QUADRANTS):
            queue = nc.sync if q % 2 == 0 else nc.scalar
            queue.dma_start(out_2[0, 4 * q : 4 * q + 4, :].bitcast(I32), out_plane[32 * q : 32 * q + 4, :].bitcast(I32))
